import numpy as np
import ml_dtypes


def mxq(x, axis, fmt="e4m3"):
    dtype, down = {"e4m3": (ml_dtypes.float8_e4m3fn, 7), "e5m2": (ml_dtypes.float8_e5m2, 14)}[fmt]
    v = np.moveaxis(np.asarray(x, np.float32).astype(ml_dtypes.bfloat16).astype(np.float64), axis, -1)
    blocks = v.reshape(v.shape[:-1] + (-1, 32))
    amax = np.abs(blocks).max(-1, keepdims=True)
    byte = np.maximum(np.where(amax > 0, np.frexp(amax)[1] - 1 + 127, 0) - down, 1)
    scale = np.exp2(byte - 127.0)
    codes = (blocks / scale).astype(np.float32).astype(dtype).astype(np.float64)
    return np.moveaxis((codes * scale).reshape(v.shape), -1, axis)


WIDE = False


def mx_kscale(k):
    if not WIDE:
        return np.ones(k)
    levels = np.array([10, -10, 5, -5, 0])
    if k % 512:
        return np.exp2(np.random.permutation(np.resize(levels, k // 32))).repeat(32)
    a = np.empty((k // 512, 16))
    for p in range(k // 512):
        a[p, :8] = np.random.permutation(np.resize(levels, 8))
        for g in range(8):
            far = levels[np.abs(levels - a[p, g]) >= 10]
            a[p, g + 8] = far[np.random.randint(len(far))]
    return np.exp2(a.ravel()).repeat(32)


BF16 = ml_dtypes.bfloat16


def bf(x):
    return np.asarray(x, np.float32).astype(BF16)


def f64(x):
    return np.asarray(x).astype(np.float64)


E2M1 = np.array([0.0, 0.5, 1.0, 1.5, 2.0, 3.0, 4.0, 6.0, -0.0, -0.5, -1.0, -1.5, -2.0, -3.0, -4.0, -6.0])


def pack_weight(w, fmt):
    k, n = w.shape
    w = f64(bf(w)).reshape(k // 32, 32, n)
    amax = np.abs(w).max(1)
    if fmt == "e4m3":
        byte = np.frexp(amax)[1] - 1 + 127 - 7
    else:
        mant, ex = np.frexp(amax / 6.0)
        byte = np.where(mant > 0.5, ex, ex - 1) + 127
    byte = np.clip(np.where(amax > 0, byte, 1), 1, 254)
    scaled = (w * np.exp2(127.0 - byte)[:, None, :]).reshape(k, n).astype(np.float32)
    by_word = np.ascontiguousarray(scaled.reshape(k // 512, 128, 4, n).transpose(0, 1, 3, 2))
    if fmt == "e4m3":
        words = by_word.astype(ml_dtypes.float8_e4m3fn).view(np.uint8)
    else:
        c = by_word.astype(ml_dtypes.float4_e2m1fn).view(np.uint8) & 0xF
        words = c[..., 0::2] | (c[..., 1::2] << 4)
    return np.ascontiguousarray(words), np.ascontiguousarray(byte.astype(np.uint8).reshape(k // 512, 16, n))


def unpack_weight(words, scales, fmt):
    g, p, n, _ = words.shape
    if fmt == "e4m3":
        vals = np.ascontiguousarray(words).view(ml_dtypes.float8_e4m3fn).astype(np.float64)
    else:
        nib = np.empty((g, p, n, 4), np.uint8)
        nib[..., 0::2] = words & 0xF
        nib[..., 1::2] = words >> 4
        vals = E2M1[nib]
    vals = vals * np.repeat(np.exp2(scales.astype(np.float64) - 127.0), 8, axis=1)[..., None]
    return vals.transpose(0, 1, 3, 2).reshape(g * 512, n)
def pack4(w):
    words, scales = pack_weight(w, "e2m1")
    return words.reshape(words.shape[0], 128, -1), scales


def unpack4(words, scales):
    return unpack_weight(words.reshape(words.shape[0], 128, -1, 2), scales, "e2m1")


M, K, J, F, N = 1024, 1024, 512, 1024, 2048

DUTY, LEAK = 0.0625, 0.06


def setup_inputs():
    s = mx_kscale(K)
    u = mx_kscale(J)
    t = mx_kscale(F)
    swerling = np.sqrt(np.random.exponential(1.0, (M, 1)))
    echo = swerling * np.random.standard_normal((M, K))
    cancel = np.random.standard_normal((J, F)) * np.sqrt(0.5 / J)
    window = (np.random.rand(F, N) < DUTY) + LEAK * np.random.rand(F, N)
    window = window / (F * (DUTY + LEAK / 2))
    cancel_words, cancel_scales = pack4(cancel / u[:, None])
    window_words, window_scales = pack4(window / t[:, None])
    return {"echo": bf(echo * s),
            "filt": bf(np.random.standard_normal((K, F)) * np.sqrt(0.5 / K) / s[:, None]),
            "aux": bf(np.random.standard_normal((M, J)) * u),
            "cancel_words": cancel_words, "cancel_scales": cancel_scales,
            "gain": bf((0.25 + 1.5 * np.random.rand(F)) * t),
            "window_words": window_words, "window_scales": window_scales,
            "rate": bf(0.75 + 0.5 * np.random.rand(N))}


def reference(echo, filt, aux, cancel_words, cancel_scales, gain, window_words, window_scales, rate):
    main = mxq(f64(echo), 1, "e4m3") @ mxq(f64(filt), 0, "e4m3")
    side = mxq(f64(aux), 1, "e4m3") @ unpack4(cancel_words, cancel_scales)
    v = main + side
    d = np.square(v) * f64(gain)
    z = mxq(d, 1, "e4m3") @ unpack4(window_words, window_scales)
    return np.exp(-(z * f64(rate)))

@@ -1,0 +1,326 @@
+from contextlib import ExitStack
+
+import concourse.mybir as mybir
+from concourse.masks import make_identity
+
+M, K, J, F, N = 1024, 1024, 512, 1024, 2048
+FLOPS = 2 * M * (K + J) * F + 2 * M * F * N
+
+F32 = mybir.dt.float32
+BF16 = mybir.dt.bfloat16
+U32 = mybir.dt.uint32
+I32 = mybir.dt.int32
+U8 = mybir.dt.uint8
+FP8X4 = mybir.dt.float8_e4m3fn_x4
+FP4X4 = mybir.dt.float4_e2m1fn_x4
+ACT = mybir.ActivationFunctionType
+MULT = mybir.AluOpType.mult
+
+P = 128
+PASS = 512
+BANK = 512
+TILES = M // P
+
+
+def tile_noncoherent_integration_map_s3_kernel(
+    tc, echo, filt, aux, cancel_words, cancel_scales, gain, window_words, window_scales, rate, out
+):
+    nc = tc.nc
+    with ExitStack() as ctx:
+        keep = ctx.enter_context(tc.tile_pool(name="keep", bufs=1))
+        work = ctx.enter_context(tc.tile_pool(name="work", bufs=3))
+        psum = ctx.enter_context(tc.psum_pool(name="psum", bufs=8))
+        ctx.enter_context(tc.manual_schedule())
+
+        ident = keep.tile([P, P], F32, name="ident")
+        make_identity(nc, ident[:])
+
+        c_plane = keep.tile([P, F], U8, name="c_plane", align_bytes=64)
+        w_plane = keep.tile([P, 2, N], U8, name="w_plane", align_bytes=64)
+        nc.vector.memset(c_plane[:].bitcast(I32), 0)
+        nc.vector.memset(w_plane[:].rearrange("p g n -> p (g n)").bitcast(I32), 0)
+        warm = keep.tile([P, 1], F32, name="warm")
+        nc.vector.memset(warm[:], 0.0)
+
+        filt_raw, echo_raw, aux_raw = {}, {}, {}
+
+        def load_filt(g, h):
+            raw = keep.tile([P, 4, PASS], BF16, name="filt_raw_%d_%d" % (g, h))
+            rows = filt[g * PASS : (g + 1) * PASS, h * PASS : (h + 1) * PASS]
+            nc.sync.dma_start(out=raw[:], in_=rows.rearrange("(p j) c -> p j c", j=4))
+            filt_raw[g, h] = raw
+
+        def load_cells(i):
+            e = keep.tile([P, K], BF16, name="echo_raw_%d" % i)
+            a = keep.tile([P, J], BF16, name="aux_raw_%d" % i)
+            nc.sync.dma_start(out=e[:], in_=echo[i * P : (i + 1) * P, :])
+            nc.sync.dma_start(out=a[:], in_=aux[i * P : (i + 1) * P, :])
+            echo_raw[i], aux_raw[i] = e, a
+
+        load_filt(0, 0)
+        for q in range(4):
+            nc.scalar.dma_start(
+                out=c_plane[32 * q : 32 * q + 4, :].bitcast(I32),
+                in_=cancel_scales[0, 4 * q : 4 * q + 4, :].bitcast(I32),
+            )
+        nc.scalar.activation(out=warm[:], in_=warm[:], func=ACT.Exp)
+        load_cells(0)
+        load_filt(1, 0)
+        c_raw = keep.tile([P, 2 * F], U8, name="c_raw")
+        nc.sync.dma_start(out=c_raw[:].bitcast(I32), in_=cancel_words[0].bitcast(I32))
+        load_cells(1)
+        load_cells(2)
+        load_filt(0, 1)
+        load_cells(3)
+        load_filt(1, 1)
+        gain_t = keep.tile([P, 2, 4], BF16, name="gain_t")
+        nc.sync.dma_start(out=gain_t[:], in_=gain.rearrange("(h p t) -> p h t", h=2, t=4))
+        load_cells(4)
+        load_cells(5)
+        for q in range(4):
+            nc.sync.dma_start(
+                out=w_plane[32 * q : 32 * q + 4].bitcast(I32),
+                in_=window_scales[:, 4 * q : 4 * q + 4, :].rearrange("g r n -> r g n").bitcast(I32),
+            )
+        w_words, rate_t = [], []
+        for half in range(2):
+            w = keep.tile([P, 2, N], U8, name="w_words_%d" % half, align_bytes=64)
+            nc.sync.dma_start(
+                out=w[:].bitcast(I32),
+                in_=window_words[:, :, half * N : (half + 1) * N].rearrange("g p c -> p g c").bitcast(I32),
+            )
+            w_words.append(w)
+            r = keep.tile([P, N // 2], BF16, name="rate_%d" % half)
+            nc.sync.dma_start(out=r[:], in_=rate[half * N // 2 : (half + 1) * N // 2].partition_broadcast(P))
+            rate_t.append(r)
+        for i in range(6, TILES):
+            load_cells(i)
+
+        filt_grouped, filt_codes, filt_plane = {}, {}, {}
+
+        def group_filt(g, h, engine, t0, t1):
+            grouped = keep.tile([P, t1 - t0, P, 4], BF16, name="filt_grouped_%d_%d_%d" % (g, h, t0), align_bytes=64)
+            dst = grouped[:].rearrange("p t (a b) j -> p a t b j", b=2)
+            src = filt_raw[g, h][:].rearrange("p j (a b t) -> p a t b j", b=2, t=4)[:, :, t0:t1]
+            if engine == "vector":
+                nc.vector.tensor_copy(out=dst, in_=src)
+            else:
+                nc.scalar.copy(out=dst, in_=src)
+            filt_grouped[g, h, t0] = grouped
+
+        def quantize_filt(g, h, t0):
+            grouped = filt_grouped[g, h, t0]
+            slots = grouped.shape[1]
+            codes = keep.tile([P, slots * P], U32, name="filt_codes_%d_%d_%d" % (g, h, t0), align_bytes=64)
+            plane = keep.tile([P, slots * P], U8, name="filt_plane_%d_%d_%d" % (g, h, t0), align_bytes=64)
+            nc.vector.quantize_mx(
+                out=codes[:].bitcast(FP8X4), scales=plane[:], in_=grouped[:].rearrange("p t m j -> p (t m j)")
+            )
+            for s in range(slots):
+                filt_codes[g, h, t0 + s] = codes[:, s * P : (s + 1) * P]
+                filt_plane[g, h, t0 + s] = plane[:, s * P : (s + 1) * P]
+            if (g, h, t0) == (0, 0, 0):
+                first_codes.extend([codes, plane])
+
+        first_codes = []
+
+        def warm_up(passes):
+            codes, plane = first_codes
+            bank = psum.tile([P, BANK], F32, name="warm_bank", tag="bank")
+            for n in range(passes):
+                nc.tensor.matmul_mx(
+                    out=bank[:], lhsT=codes[:, :P].bitcast(FP8X4), lhsT_scale=plane[:, :P],
+                    rhs=codes[:].bitcast(FP8X4), rhs_scale=plane[:], start=True, stop=True,
+                )
+
+        c_words, c_sorted_plane = {}, {}
+
+        def sort_cancel(h):
+            words = keep.tile([P, 4, P, 2], U8, name="c_words_%d" % h, align_bytes=64)
+            plane = keep.tile([P, 4, P], U8, name="c_sorted_plane_%d" % h, align_bytes=64)
+            nc.vector.tensor_copy(
+                out=words[:].rearrange("p t (a m) b -> p a t m b", m=8),
+                in_=c_raw[:, 2 * PASS * h : 2 * PASS * (h + 1)].rearrange("p (a m t b) -> p a t m b", m=8, t=4, b=2),
+            )
+            nc.vector.tensor_copy(
+                out=plane[:].rearrange("p t (a m) -> p a t m", m=16),
+                in_=c_plane[:, PASS * h : PASS * (h + 1)].rearrange("p (a m t) -> p a t m", m=16, t=4),
+            )
+            c_words[h], c_sorted_plane[h] = words, plane
+
+        turned, x_grouped, x_codes, x_plane = {}, {}, {}, {}
+
+        def turn_cells(i):
+            e_bank = psum.tile([P, 2, 2, P], F32, name="e_bank", tag="bank")
+            a_bank = psum.tile([P, 1, 2, P], F32, name="a_bank", tag="bank")
+            e_words = echo_raw[i][:].bitcast(F32)
+            a_words = aux_raw[i][:].bitcast(F32)
+            for g in range(2):
+                for u in range(2):
+                    nc.tensor.transpose(e_bank[:, g, u, :], e_words[:, 256 * g + u : 256 * (g + 1) : 2], ident[:])
+            for u in range(2):
+                nc.tensor.transpose(a_bank[:, 0, u, :], a_words[:, u:256:2], ident[:])
+            turned[i] = (e_bank, a_bank)
+
+        def group_cells(i):
+            e_bank, a_bank = turned[i]
+            e_grouped = work.tile([P, 2, P, 2], F32, name="e_grouped", align_bytes=64, bufs=4)
+            a_grouped = work.tile([P, 1, P, 2], F32, name="a_grouped", align_bytes=64, bufs=4)
+            nc.scalar.copy(out=e_grouped[:], in_=e_bank[:].rearrange("p g u m -> p g m u"))
+            nc.scalar.copy(out=a_grouped[:], in_=a_bank[:].rearrange("p g u m -> p g m u"))
+            x_grouped[i] = (e_grouped, a_grouped)
+
+        def quantize_cells(i):
+            codes = work.tile([P, 3 * P], U32, name="x_codes", align_bytes=64, bufs=6)
+            plane = work.tile([P, 3 * P], U8, name="x_plane", align_bytes=64, bufs=6)
+            e_grouped, a_grouped = x_grouped[i]
+            nc.vector.quantize_mx(
+                out=codes[:, : 2 * P].bitcast(FP8X4), scales=plane[:, : 2 * P],
+                in_=e_grouped[:].rearrange("p g m u -> p (g m u)").bitcast(BF16),
+            )
+            nc.vector.quantize_mx(
+                out=codes[:, 2 * P :].bitcast(FP8X4), scales=plane[:, 2 * P :],
+                in_=a_grouped[:].rearrange("p g m u -> p (g m u)").bitcast(BF16),
+            )
+            x_codes[i], x_plane[i] = codes, plane
+
+        volts, power, detected, d_codes, d_plane = {}, {}, {}, {}, {}
+
+        def form_volts(i, h):
+            bank = psum.tile([P, 4, P], F32, name="v_bank", tag="bank")
+            for t in range(4):
+                for g in range(2):
+                    nc.tensor.matmul_mx(
+                        out=bank[:, t, :],
+                        lhsT=filt_codes[g, h, t].bitcast(FP8X4), lhsT_scale=filt_plane[g, h, t],
+                        rhs=x_codes[i][:, g * P : (g + 1) * P].bitcast(FP8X4), rhs_scale=x_plane[i][:, g * P : (g + 1) * P],
+                        start=(g == 0), stop=False,
+                    )
+                nc.tensor.matmul_mx(
+                    out=bank[:, t, :],
+                    lhsT=c_words[h][:, t].rearrange("p m b -> p (m b)").bitcast(FP4X4), lhsT_scale=c_sorted_plane[h][:, t, :],
+                    rhs=x_codes[i][:, 2 * P :].bitcast(FP8X4), rhs_scale=x_plane[i][:, 2 * P :],
+                    start=False, stop=True,
+                )
+            volts[i, h] = bank
+
+        def square(i, h):
+            sq = work.tile([P, P, 4], F32, name="power", bufs=8)
+            nc.scalar.activation(out=sq[:], in_=volts[i, h][:].rearrange("p t m -> p m t"), func=ACT.Square)
+            power[i, h] = sq
+
+        def weigh(i, h):
+            d = work.tile([P, P, 4], BF16, name="detected", align_bytes=64)
+            nc.vector.tensor_tensor(
+                out=d[:], in0=power[i, h][:], in1=gain_t[:, h : h + 1, :].to_broadcast([P, P, 4]), op=MULT
+            )
+            detected[i, h] = d
+
+        def quantize_detected(i, h):
+            codes = work.tile([P, P], U32, name="d_codes", align_bytes=64, bufs=8)
+            plane = work.tile([P, P], U8, name="d_plane", align_bytes=64, bufs=8)
+            nc.vector.quantize_mx(
+                out=codes[:].bitcast(FP8X4), scales=plane[:], in_=detected[i, h][:].rearrange("p m t -> p (m t)")
+            )
+            d_codes[i, h], d_plane[i, h] = codes, plane
+
+        sums, scaled = {}, {}
+
+        def integrate(i, b):
+            bank = psum.tile([P, BANK], F32, name="z_bank", tag="bank")
+            for h in range(2):
+                nc.tensor.matmul_mx(
+                    out=bank[:],
+                    lhsT=d_codes[i, h][:].bitcast(FP8X4), lhsT_scale=d_plane[i, h][:],
+                    rhs=w_words[b // 2][:, h, 2 * BANK * (b % 2) : 2 * BANK * (b % 2 + 1)].bitcast(FP4X4),
+                    rhs_scale=w_plane[:, h, BANK * b : BANK * (b + 1)],
+                    start=(h == 0), stop=(h == 1),
+                )
+            sums[i, b] = bank
+
+        def apply_rate(i, b):
+            y = work.tile([P, BANK], F32, name="scaled", bufs=4)
+            nc.vector.tensor_tensor(out=y[:], in0=sums[i, b][:], in1=rate_t[b // 2][:, BANK * (b % 2) : BANK * (b % 2 + 1)], op=MULT)
+            scaled[i, b] = y
+
+        def score(i, b):
+            s = work.tile([P, BANK], F32, name="score", bufs=8)
+            nc.scalar.activation(out=s[:], in_=scaled[i, b][:], func=ACT.Exp, scale=-1.0)
+            nc.sync.dma_start(out=out[i * P : (i + 1) * P, BANK * b : BANK * (b + 1)], in_=s[:])
+
+        def volts_and_power(i, h):
+            form_volts(i, h)
+            square(i, h)
+
+        def turn_and_group(*tiles):
+            for i in tiles:
+                turn_cells(i)
+            for i in tiles:
+                group_cells(i)
+
+        def detect(i, h):
+            weigh(i, h)
+            quantize_detected(i, h)
+
+        group_filt(0, 0, "vector", 0, 4)
+        turn_and_group(0)
+        quantize_filt(0, 0, 0)
+        group_filt(1, 0, "vector", 0, 4)
+        warm_up(3)
+        turn_and_group(1)
+        quantize_cells(0)
+        quantize_filt(1, 0, 0)
+        sort_cancel(0)
+        warm_up(2)
+        turn_and_group(2)
+        quantize_cells(1)
+        group_filt(0, 1, "vector", 0, 4)
+        volts_and_power(0, 0)
+        turn_and_group(3)
+        quantize_cells(2)
+        quantize_filt(0, 1, 0)
+        volts_and_power(1, 0)
+        group_filt(1, 1, "scalar", 0, 2)
+        group_filt(1, 1, "vector", 2, 4)
+        sort_cancel(1)
+        quantize_filt(1, 1, 2)
+        quantize_cells(3)
+        quantize_filt(1, 1, 0)
+        volts_and_power(2, 0)
+        turn_and_group(4, 5)
+        volts_and_power(0, 1)
+        weigh(0, 0)
+        weigh(1, 0)
+        quantize_detected(0, 0)
+        quantize_detected(1, 0)
+        volts_and_power(3, 0)
+        volts_and_power(1, 1)
+        weigh(0, 1)
+        weigh(2, 0)
+        quantize_detected(0, 1)
+        quantize_detected(2, 0)
+        quantize_cells(4)
+
+        front = [(2, 1), (4, 0), "turn", (3, 1), (5, 0), (4, 1), (6, 0), (5, 1), (7, 0), (6, 1), (7, 1)]
+        weighs = [(1, 1), (3, 0)] + front
+        quants = {1: 5, 4: 6, 6: 7}
+        for n in range(2 * TILES):
+            i, b = n // 2, 2 * (n % 2)
+            item = front[n] if n < len(front) else None
+            w = weighs[n] if n < len(weighs) and weighs[n] != "turn" else None
+            integrate(i, b)
+            integrate(i, b + 1)
+            if w:
+                weigh(*w)
+            apply_rate(i, b)
+            if w:
+                quantize_detected(*w)
+            if n in quants:
+                quantize_cells(quants[n])
+            apply_rate(i, b + 1)
+            score(i, b)
+            if item == "turn":
+                turn_and_group(6, 7)
+            elif item:
+                volts_and_power(*item)
+            score(i, b + 1)

@@ -17,9 +17,14 @@ ACT = mybir.ActivationFunctionType
 MULT = mybir.AluOpType.mult
 
 P = 128
-PASS = 512
+SLOTS = 4
+PASS = P * SLOTS
 BANK = 512
 TILES = M // P
+AUX = 2
+FIRST_PRESORTED = 4
+TURN_STEP = 2
+LAG = 2
 
 
 def tile_noncoherent_integration_map_s3_kernel(
@@ -35,186 +40,168 @@ def tile_noncoherent_integration_map_s3_kernel(
         ident = keep.tile([P, P], F32, name="ident")
         make_identity(nc, ident[:])
 
+        table_preload = keep.tile([P, 1], F32, name="table_preload")
+        nc.scalar.activation(out=table_preload[:], in_=ident[:, :1], func=ACT.Exp)
+
         c_plane = keep.tile([P, F], U8, name="c_plane", align_bytes=64)
         w_plane = keep.tile([P, 2, N], U8, name="w_plane", align_bytes=64)
         nc.vector.memset(c_plane[:].bitcast(I32), 0)
-        nc.vector.memset(w_plane[:].rearrange("p g n -> p (g n)").bitcast(I32), 0)
-        warm = keep.tile([P, 1], F32, name="warm")
-        nc.vector.memset(warm[:], 0.0)
+        nc.vector.memset(w_plane[:].rearrange("p h n -> p (h n)").bitcast(I32), 0)
 
-        filt_raw, echo_raw, aux_raw = {}, {}, {}
+        filt_raw, echo_raw, aux_raw, w_words = {}, {}, {}, []
+
+        def load_tile(i):
+            echo_raw[i] = keep.tile([P, K], BF16, name="echo_raw_%d" % i)
+            aux_raw[i] = keep.tile([P, J], BF16, name="aux_raw_%d" % i)
+            nc.sync.dma_start(out=echo_raw[i][:], in_=echo[i * P : (i + 1) * P, :])
+            nc.sync.dma_start(out=aux_raw[i][:], in_=aux[i * P : (i + 1) * P, :])
 
         def load_filt(g, h):
-            raw = keep.tile([P, 4, PASS], BF16, name="filt_raw_%d_%d" % (g, h))
-            rows = filt[g * PASS : (g + 1) * PASS, h * PASS : (h + 1) * PASS]
-            nc.sync.dma_start(out=raw[:], in_=rows.rearrange("(p j) c -> p j c", j=4))
+            raw = keep.tile([P, SLOTS, PASS], BF16, name="filt_raw_%d_%d" % (g, h))
+            quarter = filt[g * PASS : (g + 1) * PASS, h * PASS : (h + 1) * PASS]
+            nc.sync.dma_start(out=raw[:], in_=quarter.rearrange("(p j) c -> p j c", j=SLOTS))
             filt_raw[g, h] = raw
 
-        def load_cells(i):
-            e = keep.tile([P, K], BF16, name="echo_raw_%d" % i)
-            a = keep.tile([P, J], BF16, name="aux_raw_%d" % i)
-            nc.sync.dma_start(out=e[:], in_=echo[i * P : (i + 1) * P, :])
-            nc.sync.dma_start(out=a[:], in_=aux[i * P : (i + 1) * P, :])
-            echo_raw[i], aux_raw[i] = e, a
-
+        rate_rows = keep.tile([P, N // P], BF16, name="rate_rows")
+        nc.sync.dma_start(out=rate_rows[:], in_=rate.rearrange("(p m) -> p m", p=P))
         load_filt(0, 0)
+        load_tile(0)
+        load_filt(1, 0)
         for q in range(4):
-            nc.scalar.dma_start(
+            nc.sync.dma_start(
                 out=c_plane[32 * q : 32 * q + 4, :].bitcast(I32),
                 in_=cancel_scales[0, 4 * q : 4 * q + 4, :].bitcast(I32),
             )
-        nc.scalar.activation(out=warm[:], in_=warm[:], func=ACT.Exp)
-        load_cells(0)
-        load_filt(1, 0)
         c_raw = keep.tile([P, 2 * F], U8, name="c_raw")
         nc.sync.dma_start(out=c_raw[:].bitcast(I32), in_=cancel_words[0].bitcast(I32))
-        load_cells(1)
-        load_cells(2)
+        load_tile(1)
+        load_tile(2)
         load_filt(0, 1)
-        load_cells(3)
+        load_tile(3)
         load_filt(1, 1)
-        gain_t = keep.tile([P, 2, 4], BF16, name="gain_t")
-        nc.sync.dma_start(out=gain_t[:], in_=gain.rearrange("(h p t) -> p h t", h=2, t=4))
-        load_cells(4)
-        load_cells(5)
+        gain_t = keep.tile([P, 2, SLOTS], BF16, name="gain_t")
+        nc.sync.dma_start(out=gain_t[:], in_=gain.rearrange("(h p t) -> p h t", h=2, t=SLOTS))
+        load_tile(4)
+        load_tile(5)
         for q in range(4):
             nc.sync.dma_start(
                 out=w_plane[32 * q : 32 * q + 4].bitcast(I32),
-                in_=window_scales[:, 4 * q : 4 * q + 4, :].rearrange("g r n -> r g n").bitcast(I32),
+                in_=window_scales[:, 4 * q : 4 * q + 4, :].rearrange("h r n -> r h n").bitcast(I32),
             )
-        w_words, rate_t = [], []
         for half in range(2):
-            w = keep.tile([P, 2, N], U8, name="w_words_%d" % half, align_bytes=64)
+            words = keep.tile([P, 2, N], U8, name="w_words_%d" % half, align_bytes=64)
             nc.sync.dma_start(
-                out=w[:].bitcast(I32),
-                in_=window_words[:, :, half * N : (half + 1) * N].rearrange("g p c -> p g c").bitcast(I32),
+                out=words[:].bitcast(I32),
+                in_=window_words[:, :, half * N : (half + 1) * N].rearrange("h p c -> p h c").bitcast(I32),
             )
-            w_words.append(w)
-            r = keep.tile([P, N // 2], BF16, name="rate_%d" % half)
-            nc.sync.dma_start(out=r[:], in_=rate[half * N // 2 : (half + 1) * N // 2].partition_broadcast(P))
-            rate_t.append(r)
-        for i in range(6, TILES):
-            load_cells(i)
+            w_words.append(words)
+        load_tile(6)
+        load_tile(7)
 
-        filt_grouped, filt_codes, filt_plane = {}, {}, {}
+        rate_words = keep.tile([P, P, 2, 4], F32, name="rate_words")
+        rate_all = rate_words[:].rearrange("q p s j -> q (p s j)").bitcast(BF16)
 
-        def group_filt(g, h, engine, t0, t1):
-            grouped = keep.tile([P, t1 - t0, P, 4], BF16, name="filt_grouped_%d_%d_%d" % (g, h, t0), align_bytes=64)
-            dst = grouped[:].rearrange("p t (a b) j -> p a t b j", b=2)
-            src = filt_raw[g, h][:].rearrange("p j (a b t) -> p a t b j", b=2, t=4)[:, :, t0:t1]
-            if engine == "vector":
-                nc.vector.tensor_copy(out=dst, in_=src)
-            else:
-                nc.scalar.copy(out=dst, in_=src)
-            filt_grouped[g, h, t0] = grouped
+        def spread_rate():
+            pairs = rate_rows[:].bitcast(F32)
+            for s in range(2):
+                bank = psum.tile([P, 4, P], F32, name="rate_bank", tag="bank")
+                for j in range(4):
+                    column = pairs[:, 4 * s + j : 4 * s + j + 1]
+                    nc.tensor.transpose(bank[:, j, :], column.to_broadcast([P, P]), ident[:])
+                nc.scalar.copy(out=rate_words[:, :, s, :], in_=bank[:].rearrange("q j p -> q p j"))
 
-        def quantize_filt(g, h, t0):
-            grouped = filt_grouped[g, h, t0]
-            slots = grouped.shape[1]
-            codes = keep.tile([P, slots * P], U32, name="filt_codes_%d_%d_%d" % (g, h, t0), align_bytes=64)
-            plane = keep.tile([P, slots * P], U8, name="filt_plane_%d_%d_%d" % (g, h, t0), align_bytes=64)
+        stationary, filt_grouped = {}, {}
+
+        def group_filt(g, h):
+            grouped = keep.tile([P, SLOTS, P, SLOTS], BF16, name="filt_grouped_%d_%d" % (g, h), align_bytes=64)
+            nc.vector.tensor_copy(
+                out=grouped[:].rearrange("p t (a b) j -> p a t b j", b=2),
+                in_=filt_raw[g, h][:].rearrange("p j (a b t) -> p a t b j", b=2, t=SLOTS),
+            )
+            filt_grouped[g, h] = grouped
+
+        def quantize_filt(g, h):
+            codes = keep.tile([P, PASS], U32, name="filt_codes_%d_%d" % (g, h), align_bytes=64)
+            plane = keep.tile([P, PASS], U8, name="filt_plane_%d_%d" % (g, h), align_bytes=64)
             nc.vector.quantize_mx(
-                out=codes[:].bitcast(FP8X4), scales=plane[:], in_=grouped[:].rearrange("p t m j -> p (t m j)")
+                out=codes[:].bitcast(FP8X4), scales=plane[:],
+                in_=filt_grouped[g, h][:].rearrange("p t m j -> p (t m j)"),
             )
-            for s in range(slots):
-                filt_codes[g, h, t0 + s] = codes[:, s * P : (s + 1) * P]
-                filt_plane[g, h, t0 + s] = plane[:, s * P : (s + 1) * P]
-            if (g, h, t0) == (0, 0, 0):
-                first_codes.extend([codes, plane])
-
-        first_codes = []
-
-        def warm_up(passes):
-            codes, plane = first_codes
-            bank = psum.tile([P, BANK], F32, name="warm_bank", tag="bank")
-            for n in range(passes):
-                nc.tensor.matmul_mx(
-                    out=bank[:], lhsT=codes[:, :P].bitcast(FP8X4), lhsT_scale=plane[:, :P],
-                    rhs=codes[:].bitcast(FP8X4), rhs_scale=plane[:], start=True, stop=True,
-                )
-
-        c_words, c_sorted_plane = {}, {}
+            for t in range(SLOTS):
+                columns = slice(t * P, (t + 1) * P)
+                stationary[g, h, t] = (codes[:, columns].bitcast(FP8X4), plane[:, columns])
 
         def sort_cancel(h):
-            words = keep.tile([P, 4, P, 2], U8, name="c_words_%d" % h, align_bytes=64)
-            plane = keep.tile([P, 4, P], U8, name="c_sorted_plane_%d" % h, align_bytes=64)
+            words = keep.tile([P, SLOTS, P, 2], U8, name="c_words_%d" % h, align_bytes=64)
+            plane = keep.tile([P, SLOTS, P], U8, name="c_sorted_plane_%d" % h, align_bytes=64)
             nc.vector.tensor_copy(
                 out=words[:].rearrange("p t (a m) b -> p a t m b", m=8),
-                in_=c_raw[:, 2 * PASS * h : 2 * PASS * (h + 1)].rearrange("p (a m t b) -> p a t m b", m=8, t=4, b=2),
+                in_=c_raw[:, 2 * PASS * h : 2 * PASS * (h + 1)].rearrange("p (a m t b) -> p a t m b", m=8, t=SLOTS, b=2),
             )
             nc.vector.tensor_copy(
                 out=plane[:].rearrange("p t (a m) -> p a t m", m=16),
-                in_=c_plane[:, PASS * h : PASS * (h + 1)].rearrange("p (a m t) -> p a t m", m=16, t=4),
+                in_=c_plane[:, PASS * h : PASS * (h + 1)].rearrange("p (a m t) -> p a t m", m=16, t=SLOTS),
             )
-            c_words[h], c_sorted_plane[h] = words, plane
+            for t in range(SLOTS):
+                stationary[AUX, h, t] = (words[:, t].rearrange("p m b -> p (m b)").bitcast(FP4X4), plane[:, t, :])
 
-        turned, x_grouped, x_codes, x_plane = {}, {}, {}, {}
+        sample_words, x_grouped, x_codes, x_plane = {}, {}, {}, {}
 
-        def turn_cells(i):
-            e_bank = psum.tile([P, 2, 2, P], F32, name="e_bank", tag="bank")
-            a_bank = psum.tile([P, 1, 2, P], F32, name="a_bank", tag="bank")
-            e_words = echo_raw[i][:].bitcast(F32)
-            a_words = aux_raw[i][:].bitcast(F32)
-            for g in range(2):
-                for u in range(2):
-                    nc.tensor.transpose(e_bank[:, g, u, :], e_words[:, 256 * g + u : 256 * (g + 1) : 2], ident[:])
-            for u in range(2):
-                nc.tensor.transpose(a_bank[:, 0, u, :], a_words[:, u:256:2], ident[:])
-            turned[i] = (e_bank, a_bank)
+        def words_by_parity(raw):
+            return raw[:].bitcast(F32).rearrange("m (g p u) -> m g u p", p=P, u=2)
 
-        def group_cells(i):
-            e_bank, a_bank = turned[i]
-            e_grouped = work.tile([P, 2, P, 2], F32, name="e_grouped", align_bytes=64, bufs=4)
-            a_grouped = work.tile([P, 1, P, 2], F32, name="a_grouped", align_bytes=64, bufs=4)
-            nc.scalar.copy(out=e_grouped[:], in_=e_bank[:].rearrange("p g u m -> p g m u"))
-            nc.scalar.copy(out=a_grouped[:], in_=a_bank[:].rearrange("p g u m -> p g m u"))
-            x_grouped[i] = (e_grouped, a_grouped)
+        def presort(i):
+            copies = []
+            for raw, name in ((echo_raw[i], "echo_sorted"), (aux_raw[i], "aux_sorted")):
+                view = words_by_parity(raw)
+                ordered = work.tile(list(view.shape), F32, name=name)
+                nc.scalar.copy(out=ordered[:], in_=view)
+                copies.append(ordered[:])
+            sample_words[i] = copies
+
+        def turn(*tiles):
+            banks = []
+            for i in tiles:
+                if i < FIRST_PRESORTED:
+                    sample_words[i] = [words_by_parity(echo_raw[i]), words_by_parity(aux_raw[i])]
+                for words in sample_words[i]:
+                    bank = psum.tile(list(words.shape), F32, name="turn_bank", tag="bank")
+                    for g in range(words.shape[1]):
+                        for u in range(2):
+                            nc.tensor.transpose(bank[:, g, u, :], words[:, g, u, :], ident[:])
+                    banks.append((i, bank))
+            for i, bank in banks:
+                grouped = work.tile([P, bank.shape[1], P, 2], F32, name="x_grouped", align_bytes=64, bufs=8)
+                nc.scalar.copy(out=grouped[:], in_=bank[:].rearrange("p g u m -> p g m u"))
+                x_grouped.setdefault(i, []).append(grouped[:].rearrange("p g m u -> p (g m u)").bitcast(BF16))
 
         def quantize_cells(i):
-            codes = work.tile([P, 3 * P], U32, name="x_codes", align_bytes=64, bufs=6)
-            plane = work.tile([P, 3 * P], U8, name="x_plane", align_bytes=64, bufs=6)
-            e_grouped, a_grouped = x_grouped[i]
-            nc.vector.quantize_mx(
-                out=codes[:, : 2 * P].bitcast(FP8X4), scales=plane[:, : 2 * P],
-                in_=e_grouped[:].rearrange("p g m u -> p (g m u)").bitcast(BF16),
-            )
-            nc.vector.quantize_mx(
-                out=codes[:, 2 * P :].bitcast(FP8X4), scales=plane[:, 2 * P :],
-                in_=a_grouped[:].rearrange("p g m u -> p (g m u)").bitcast(BF16),
-            )
+            codes = work.tile([P, (AUX + 1) * P], U32, name="x_codes", align_bytes=64, bufs=6)
+            plane = work.tile([P, (AUX + 1) * P], U8, name="x_plane", align_bytes=64, bufs=6)
+            for columns, grouped in zip((slice(0, AUX * P), slice(AUX * P, (AUX + 1) * P)), x_grouped[i]):
+                nc.vector.quantize_mx(out=codes[:, columns].bitcast(FP8X4), scales=plane[:, columns], in_=grouped)
             x_codes[i], x_plane[i] = codes, plane
 
-        volts, power, detected, d_codes, d_plane = {}, {}, {}, {}, {}
+        power, detected, d_codes, d_plane = {}, {}, {}, {}
 
-        def form_volts(i, h):
-            bank = psum.tile([P, 4, P], F32, name="v_bank", tag="bank")
-            for t in range(4):
-                for g in range(2):
+        def volts_squared(i, h):
+            bank = psum.tile([P, SLOTS, P], F32, name="v_bank", tag="bank")
+            for t in range(SLOTS):
+                for g in range(AUX + 1):
+                    cells = slice(g * P, (g + 1) * P)
+                    weights, weights_plane = stationary[g, h, t]
                     nc.tensor.matmul_mx(
-                        out=bank[:, t, :],
-                        lhsT=filt_codes[g, h, t].bitcast(FP8X4), lhsT_scale=filt_plane[g, h, t],
-                        rhs=x_codes[i][:, g * P : (g + 1) * P].bitcast(FP8X4), rhs_scale=x_plane[i][:, g * P : (g + 1) * P],
-                        start=(g == 0), stop=False,
+                        out=bank[:, t, :], lhsT=weights, lhsT_scale=weights_plane,
+                        rhs=x_codes[i][:, cells].bitcast(FP8X4), rhs_scale=x_plane[i][:, cells],
+                        start=(g == 0), stop=(g == AUX),
                     )
-                nc.tensor.matmul_mx(
-                    out=bank[:, t, :],
-                    lhsT=c_words[h][:, t].rearrange("p m b -> p (m b)").bitcast(FP4X4), lhsT_scale=c_sorted_plane[h][:, t, :],
-                    rhs=x_codes[i][:, 2 * P :].bitcast(FP8X4), rhs_scale=x_plane[i][:, 2 * P :],
-                    start=False, stop=True,
-                )
-            volts[i, h] = bank
-
-        def square(i, h):
-            sq = work.tile([P, P, 4], F32, name="power", bufs=8)
-            nc.scalar.activation(out=sq[:], in_=volts[i, h][:].rearrange("p t m -> p m t"), func=ACT.Square)
-            power[i, h] = sq
+            power[i, h] = work.tile([P, P, SLOTS], F32, name="power", bufs=8)
+            nc.scalar.activation(out=power[i, h][:], in_=bank[:].rearrange("p t m -> p m t"), func=ACT.Square)
 
         def weigh(i, h):
-            d = work.tile([P, P, 4], BF16, name="detected", align_bytes=64)
-            nc.vector.tensor_tensor(
-                out=d[:], in0=power[i, h][:], in1=gain_t[:, h : h + 1, :].to_broadcast([P, P, 4]), op=MULT
-            )
-            detected[i, h] = d
+            detected[i, h] = work.tile([P, P, SLOTS], BF16, name="detected", align_bytes=64)
+            factors = gain_t[:, h : h + 1, :].to_broadcast([P, P, SLOTS])
+            nc.vector.tensor_tensor(out=detected[i, h][:], in0=power[i, h][:], in1=factors, op=MULT)
 
         def quantize_detected(i, h):
             codes = work.tile([P, P], U32, name="d_codes", align_bytes=64, bufs=8)
@@ -223,8 +210,6 @@ def tile_noncoherent_integration_map_s3_kernel(
                 out=codes[:].bitcast(FP8X4), scales=plane[:], in_=detected[i, h][:].rearrange("p m t -> p (m t)")
             )
             d_codes[i, h], d_plane[i, h] = codes, plane
-
-        sums, scaled = {}, {}
 
         def integrate(i, b):
             bank = psum.tile([P, BANK], F32, name="z_bank", tag="bank")
@@ -236,91 +221,90 @@ def tile_noncoherent_integration_map_s3_kernel(
                     rhs_scale=w_plane[:, h, BANK * b : BANK * (b + 1)],
                     start=(h == 0), stop=(h == 1),
                 )
-            sums[i, b] = bank
+            return bank
 
-        def apply_rate(i, b):
-            y = work.tile([P, BANK], F32, name="scaled", bufs=4)
-            nc.vector.tensor_tensor(out=y[:], in0=sums[i, b][:], in1=rate_t[b // 2][:, BANK * (b % 2) : BANK * (b % 2 + 1)], op=MULT)
-            scaled[i, b] = y
+        def apply_rate(bank, b, c0, c1):
+            scaled = work.tile([P, c1 - c0], F32, name="scaled", bufs=8)
+            windows = slice(BANK * b + c0, BANK * b + c1)
+            nc.vector.tensor_tensor(out=scaled[:], in0=bank[:, c0:c1], in1=rate_all[:, windows], op=MULT)
+            return scaled, windows
 
-        def score(i, b):
-            s = work.tile([P, BANK], F32, name="score", bufs=8)
-            nc.scalar.activation(out=s[:], in_=scaled[i, b][:], func=ACT.Exp, scale=-1.0)
-            nc.sync.dma_start(out=out[i * P : (i + 1) * P, BANK * b : BANK * (b + 1)], in_=s[:])
+        def score(i, scaled, windows):
+            result = work.tile(list(scaled.shape), F32, name="result", bufs=8)
+            nc.scalar.activation(out=result[:], in_=scaled[:], func=ACT.Exp, scale=-1.0)
+            nc.sync.dma_start(out=out[i * P : (i + 1) * P, windows], in_=result[:])
 
-        def volts_and_power(i, h):
-            form_volts(i, h)
-            square(i, h)
-
-        def turn_and_group(*tiles):
-            for i in tiles:
-                turn_cells(i)
-            for i in tiles:
-                group_cells(i)
-
-        def detect(i, h):
-            weigh(i, h)
-            quantize_detected(i, h)
-
-        group_filt(0, 0, "vector", 0, 4)
-        turn_and_group(0)
-        quantize_filt(0, 0, 0)
-        group_filt(1, 0, "vector", 0, 4)
-        warm_up(3)
-        turn_and_group(1)
+        spread_rate()
+        group_filt(0, 0)
+        turn(0)
+        quantize_filt(0, 0)
+        group_filt(1, 0)
+        turn(1)
         quantize_cells(0)
-        quantize_filt(1, 0, 0)
+        quantize_filt(1, 0)
         sort_cancel(0)
-        warm_up(2)
-        turn_and_group(2)
+        turn(2)
         quantize_cells(1)
-        group_filt(0, 1, "vector", 0, 4)
-        volts_and_power(0, 0)
-        turn_and_group(3)
+        group_filt(0, 1)
+        volts_squared(0, 0)
+        turn(3)
         quantize_cells(2)
-        quantize_filt(0, 1, 0)
-        volts_and_power(1, 0)
-        group_filt(1, 1, "scalar", 0, 2)
-        group_filt(1, 1, "vector", 2, 4)
-        sort_cancel(1)
-        quantize_filt(1, 1, 2)
+        quantize_filt(0, 1)
+        volts_squared(1, 0)
+        presort(4)
+        group_filt(1, 1)
         quantize_cells(3)
-        quantize_filt(1, 1, 0)
-        volts_and_power(2, 0)
-        turn_and_group(4, 5)
-        volts_and_power(0, 1)
+        quantize_filt(1, 1)
+        sort_cancel(1)
+        volts_squared(2, 0)
+        volts_squared(3, 0)
+        presort(5)
+        turn(4)
+        volts_squared(0, 1)
+        turn(5)
+        volts_squared(1, 1)
+        volts_squared(2, 1)
         weigh(0, 0)
         weigh(1, 0)
         quantize_detected(0, 0)
         quantize_detected(1, 0)
-        volts_and_power(3, 0)
-        volts_and_power(1, 1)
-        weigh(0, 1)
         weigh(2, 0)
-        quantize_detected(0, 1)
+        weigh(3, 0)
         quantize_detected(2, 0)
+        quantize_detected(3, 0)
+        weigh(0, 1)
         quantize_cells(4)
+        quantize_detected(0, 1)
+        quantize_cells(5)
 
-        front = [(2, 1), (4, 0), "turn", (3, 1), (5, 0), (4, 1), (6, 0), (5, 1), (7, 0), (6, 1), (7, 1)]
-        weighs = [(1, 1), (3, 0)] + front
-        quants = {1: 5, 4: 6, 6: 7}
-        for n in range(2 * TILES):
+        pieces = []
+        for i in range(3, TILES):
+            if i + 1 < TILES:
+                pieces.append((i + 1, 0))
+            pieces.append((i, 1))
+        pieces.insert(TURN_STEP, None)
+        to_weigh = [(1, 1), (2, 1)] + pieces
+        to_quantize = {TURN_STEP + LAG: TILES - 2, TURN_STEP + LAG + 1: TILES - 1}
+        steps = 2 * TILES
+        for n in range(steps):
             i, b = n // 2, 2 * (n % 2)
-            item = front[n] if n < len(front) else None
-            w = weighs[n] if n < len(weighs) and weighs[n] != "turn" else None
-            integrate(i, b)
-            integrate(i, b + 1)
-            if w:
-                weigh(*w)
-            apply_rate(i, b)
-            if w:
-                quantize_detected(*w)
-            if n in quants:
-                quantize_cells(quants[n])
-            apply_rate(i, b + 1)
-            score(i, b)
-            if item == "turn":
-                turn_and_group(6, 7)
-            elif item:
-                volts_and_power(*item)
-            score(i, b + 1)
+            first_bank, second_bank = integrate(i, b), integrate(i, b + 1)
+            weighing = to_weigh[n] if n < len(to_weigh) else None
+            if weighing:
+                weigh(*weighing)
+            first = apply_rate(first_bank, b, 0, BANK)
+            if weighing:
+                quantize_detected(*weighing)
+            if n in to_quantize:
+                quantize_cells(to_quantize[n])
+            cuts = (0, BANK) if n < steps - 1 else (0, BANK // 2, BANK)
+            second = [apply_rate(second_bank, b + 1, c0, c1) for c0, c1 in zip(cuts, cuts[1:])]
+            if n < TURN_STEP:
+                presort(TILES - TURN_STEP + n)
+            score(i, *first)
+            if n == TURN_STEP:
+                turn(TILES - 2, TILES - 1)
+            elif n < len(pieces):
+                volts_squared(*pieces[n])
+            for part in second:
+                score(i, *part)

from contextlib import ExitStack

import concourse.mybir as mybir
from concourse.masks import make_identity

M, K, J, F, N = 1024, 1024, 512, 1024, 2048
FLOPS = 2 * M * (K + J) * F + 2 * M * F * N

F32 = mybir.dt.float32
BF16 = mybir.dt.bfloat16
U32 = mybir.dt.uint32
I32 = mybir.dt.int32
U8 = mybir.dt.uint8
FP8X4 = mybir.dt.float8_e4m3fn_x4
FP4X4 = mybir.dt.float4_e2m1fn_x4
ACT = mybir.ActivationFunctionType
MULT = mybir.AluOpType.mult

P = 128
SLOTS = 4
PASS = P * SLOTS
BANK = 512
TILES = M // P
AUX = 2
FIRST_PRESORTED = 4
TURN_STEP = 2
LAG = 2


def tile_noncoherent_integration_map_s3_kernel(
    tc, echo, filt, aux, cancel_words, cancel_scales, gain, window_words, window_scales, rate, out
):
    nc = tc.nc
    with ExitStack() as ctx:
        keep = ctx.enter_context(tc.tile_pool(name="keep", bufs=1))
        work = ctx.enter_context(tc.tile_pool(name="work", bufs=3))
        psum = ctx.enter_context(tc.psum_pool(name="psum", bufs=8))
        ctx.enter_context(tc.manual_schedule())

        ident = keep.tile([P, P], F32, name="ident")
        make_identity(nc, ident[:])

        table_preload = keep.tile([P, 1], F32, name="table_preload")
        nc.scalar.activation(out=table_preload[:], in_=ident[:, :1], func=ACT.Exp)

        c_plane = keep.tile([P, F], U8, name="c_plane", align_bytes=64)
        w_plane = keep.tile([P, 2, N], U8, name="w_plane", align_bytes=64)
        nc.vector.memset(c_plane[:].bitcast(I32), 0)
        nc.vector.memset(w_plane[:].rearrange("p h n -> p (h n)").bitcast(I32), 0)

        filt_raw, echo_raw, aux_raw, w_words = {}, {}, {}, []

        def load_tile(i):
            echo_raw[i] = keep.tile([P, K], BF16, name="echo_raw_%d" % i)
            aux_raw[i] = keep.tile([P, J], BF16, name="aux_raw_%d" % i)
            nc.sync.dma_start(out=echo_raw[i][:], in_=echo[i * P : (i + 1) * P, :])
            nc.sync.dma_start(out=aux_raw[i][:], in_=aux[i * P : (i + 1) * P, :])

        def load_filt(g, h):
            raw = keep.tile([P, SLOTS, PASS], BF16, name="filt_raw_%d_%d" % (g, h))
            quarter = filt[g * PASS : (g + 1) * PASS, h * PASS : (h + 1) * PASS]
            nc.sync.dma_start(out=raw[:], in_=quarter.rearrange("(p j) c -> p j c", j=SLOTS))
            filt_raw[g, h] = raw

        rate_rows = keep.tile([P, N // P], BF16, name="rate_rows")
        nc.sync.dma_start(out=rate_rows[:], in_=rate.rearrange("(p m) -> p m", p=P))
        load_filt(0, 0)
        load_tile(0)
        load_filt(1, 0)
        for q in range(4):
            nc.sync.dma_start(
                out=c_plane[32 * q : 32 * q + 4, :].bitcast(I32),
                in_=cancel_scales[0, 4 * q : 4 * q + 4, :].bitcast(I32),
            )
        c_raw = keep.tile([P, 2 * F], U8, name="c_raw")
        nc.sync.dma_start(out=c_raw[:].bitcast(I32), in_=cancel_words[0].bitcast(I32))
        load_tile(1)
        load_tile(2)
        load_filt(0, 1)
        load_tile(3)
        load_filt(1, 1)
        gain_t = keep.tile([P, 2, SLOTS], BF16, name="gain_t")
        nc.sync.dma_start(out=gain_t[:], in_=gain.rearrange("(h p t) -> p h t", h=2, t=SLOTS))
        load_tile(4)
        load_tile(5)
        for q in range(4):
            nc.sync.dma_start(
                out=w_plane[32 * q : 32 * q + 4].bitcast(I32),
                in_=window_scales[:, 4 * q : 4 * q + 4, :].rearrange("h r n -> r h n").bitcast(I32),
            )
        for half in range(2):
            words = keep.tile([P, 2, N], U8, name="w_words_%d" % half, align_bytes=64)
            nc.sync.dma_start(
                out=words[:].bitcast(I32),
                in_=window_words[:, :, half * N : (half + 1) * N].rearrange("h p c -> p h c").bitcast(I32),
            )
            w_words.append(words)
        load_tile(6)
        load_tile(7)

        rate_words = keep.tile([P, P, 2, 4], F32, name="rate_words")
        rate_all = rate_words[:].rearrange("q p s j -> q (p s j)").bitcast(BF16)

        def spread_rate():
            pairs = rate_rows[:].bitcast(F32)
            for s in range(2):
                bank = psum.tile([P, 4, P], F32, name="rate_bank", tag="bank")
                for j in range(4):
                    column = pairs[:, 4 * s + j : 4 * s + j + 1]
                    nc.tensor.transpose(bank[:, j, :], column.to_broadcast([P, P]), ident[:])
                nc.scalar.copy(out=rate_words[:, :, s, :], in_=bank[:].rearrange("q j p -> q p j"))

        stationary, filt_grouped = {}, {}

        def group_filt(g, h):
            grouped = keep.tile([P, SLOTS, P, SLOTS], BF16, name="filt_grouped_%d_%d" % (g, h), align_bytes=64)
            nc.vector.tensor_copy(
                out=grouped[:].rearrange("p t (a b) j -> p a t b j", b=2),
                in_=filt_raw[g, h][:].rearrange("p j (a b t) -> p a t b j", b=2, t=SLOTS),
            )
            filt_grouped[g, h] = grouped

        def quantize_filt(g, h):
            codes = keep.tile([P, PASS], U32, name="filt_codes_%d_%d" % (g, h), align_bytes=64)
            plane = keep.tile([P, PASS], U8, name="filt_plane_%d_%d" % (g, h), align_bytes=64)
            nc.vector.quantize_mx(
                out=codes[:].bitcast(FP8X4), scales=plane[:],
                in_=filt_grouped[g, h][:].rearrange("p t m j -> p (t m j)"),
            )
            for t in range(SLOTS):
                columns = slice(t * P, (t + 1) * P)
                stationary[g, h, t] = (codes[:, columns].bitcast(FP8X4), plane[:, columns])

        def sort_cancel(h):
            words = keep.tile([P, SLOTS, P, 2], U8, name="c_words_%d" % h, align_bytes=64)
            plane = keep.tile([P, SLOTS, P], U8, name="c_sorted_plane_%d" % h, align_bytes=64)
            nc.vector.tensor_copy(
                out=words[:].rearrange("p t (a m) b -> p a t m b", m=8),
                in_=c_raw[:, 2 * PASS * h : 2 * PASS * (h + 1)].rearrange("p (a m t b) -> p a t m b", m=8, t=SLOTS, b=2),
            )
            nc.vector.tensor_copy(
                out=plane[:].rearrange("p t (a m) -> p a t m", m=16),
                in_=c_plane[:, PASS * h : PASS * (h + 1)].rearrange("p (a m t) -> p a t m", m=16, t=SLOTS),
            )
            for t in range(SLOTS):
                stationary[AUX, h, t] = (words[:, t].rearrange("p m b -> p (m b)").bitcast(FP4X4), plane[:, t, :])

        sample_words, x_grouped, x_codes, x_plane = {}, {}, {}, {}

        def words_by_parity(raw):
            return raw[:].bitcast(F32).rearrange("m (g p u) -> m g u p", p=P, u=2)

        def presort(i):
            copies = []
            for raw, name in ((echo_raw[i], "echo_sorted"), (aux_raw[i], "aux_sorted")):
                view = words_by_parity(raw)
                ordered = work.tile(list(view.shape), F32, name=name)
                nc.scalar.copy(out=ordered[:], in_=view)
                copies.append(ordered[:])
            sample_words[i] = copies

        def turn(*tiles):
            banks = []
            for i in tiles:
                if i < FIRST_PRESORTED:
                    sample_words[i] = [words_by_parity(echo_raw[i]), words_by_parity(aux_raw[i])]
                for words in sample_words[i]:
                    bank = psum.tile(list(words.shape), F32, name="turn_bank", tag="bank")
                    for g in range(words.shape[1]):
                        for u in range(2):
                            nc.tensor.transpose(bank[:, g, u, :], words[:, g, u, :], ident[:])
                    banks.append((i, bank))
            for i, bank in banks:
                grouped = work.tile([P, bank.shape[1], P, 2], F32, name="x_grouped", align_bytes=64, bufs=8)
                nc.scalar.copy(out=grouped[:], in_=bank[:].rearrange("p g u m -> p g m u"))
                x_grouped.setdefault(i, []).append(grouped[:].rearrange("p g m u -> p (g m u)").bitcast(BF16))

        def quantize_cells(i):
            codes = work.tile([P, (AUX + 1) * P], U32, name="x_codes", align_bytes=64, bufs=6)
            plane = work.tile([P, (AUX + 1) * P], U8, name="x_plane", align_bytes=64, bufs=6)
            for columns, grouped in zip((slice(0, AUX * P), slice(AUX * P, (AUX + 1) * P)), x_grouped[i]):
                nc.vector.quantize_mx(out=codes[:, columns].bitcast(FP8X4), scales=plane[:, columns], in_=grouped)
            x_codes[i], x_plane[i] = codes, plane

        power, detected, d_codes, d_plane = {}, {}, {}, {}

        def volts_squared(i, h):
            bank = psum.tile([P, SLOTS, P], F32, name="v_bank", tag="bank")
            for t in range(SLOTS):
                for g in range(AUX + 1):
                    cells = slice(g * P, (g + 1) * P)
                    weights, weights_plane = stationary[g, h, t]
                    nc.tensor.matmul_mx(
                        out=bank[:, t, :], lhsT=weights, lhsT_scale=weights_plane,
                        rhs=x_codes[i][:, cells].bitcast(FP8X4), rhs_scale=x_plane[i][:, cells],
                        start=(g == 0), stop=(g == AUX),
                    )
            power[i, h] = work.tile([P, P, SLOTS], F32, name="power", bufs=8)
            nc.scalar.activation(out=power[i, h][:], in_=bank[:].rearrange("p t m -> p m t"), func=ACT.Square)

        def weigh(i, h):
            detected[i, h] = work.tile([P, P, SLOTS], BF16, name="detected", align_bytes=64)
            factors = gain_t[:, h : h + 1, :].to_broadcast([P, P, SLOTS])
            nc.vector.tensor_tensor(out=detected[i, h][:], in0=power[i, h][:], in1=factors, op=MULT)

        def quantize_detected(i, h):
            codes = work.tile([P, P], U32, name="d_codes", align_bytes=64, bufs=8)
            plane = work.tile([P, P], U8, name="d_plane", align_bytes=64, bufs=8)
            nc.vector.quantize_mx(
                out=codes[:].bitcast(FP8X4), scales=plane[:], in_=detected[i, h][:].rearrange("p m t -> p (m t)")
            )
            d_codes[i, h], d_plane[i, h] = codes, plane

        def integrate(i, b):
            bank = psum.tile([P, BANK], F32, name="z_bank", tag="bank")
            for h in range(2):
                nc.tensor.matmul_mx(
                    out=bank[:],
                    lhsT=d_codes[i, h][:].bitcast(FP8X4), lhsT_scale=d_plane[i, h][:],
                    rhs=w_words[b // 2][:, h, 2 * BANK * (b % 2) : 2 * BANK * (b % 2 + 1)].bitcast(FP4X4),
                    rhs_scale=w_plane[:, h, BANK * b : BANK * (b + 1)],
                    start=(h == 0), stop=(h == 1),
                )
            return bank

        def apply_rate(bank, b, c0, c1):
            scaled = work.tile([P, c1 - c0], F32, name="scaled", bufs=8)
            windows = slice(BANK * b + c0, BANK * b + c1)
            nc.vector.tensor_tensor(out=scaled[:], in0=bank[:, c0:c1], in1=rate_all[:, windows], op=MULT)
            return scaled, windows

        def score(i, scaled, windows):
            result = work.tile(list(scaled.shape), F32, name="result", bufs=8)
            nc.scalar.activation(out=result[:], in_=scaled[:], func=ACT.Exp, scale=-1.0)
            nc.sync.dma_start(out=out[i * P : (i + 1) * P, windows], in_=result[:])

        spread_rate()
        group_filt(0, 0)
        turn(0)
        quantize_filt(0, 0)
        group_filt(1, 0)
        turn(1)
        quantize_cells(0)
        quantize_filt(1, 0)
        sort_cancel(0)
        turn(2)
        quantize_cells(1)
        group_filt(0, 1)
        volts_squared(0, 0)
        turn(3)
        quantize_cells(2)
        quantize_filt(0, 1)
        volts_squared(1, 0)
        presort(4)
        group_filt(1, 1)
        quantize_cells(3)
        quantize_filt(1, 1)
        sort_cancel(1)
        volts_squared(2, 0)
        volts_squared(3, 0)
        presort(5)
        turn(4)
        volts_squared(0, 1)
        turn(5)
        volts_squared(1, 1)
        volts_squared(2, 1)
        weigh(0, 0)
        weigh(1, 0)
        quantize_detected(0, 0)
        quantize_detected(1, 0)
        weigh(2, 0)
        weigh(3, 0)
        quantize_detected(2, 0)
        quantize_detected(3, 0)
        weigh(0, 1)
        quantize_cells(4)
        quantize_detected(0, 1)
        quantize_cells(5)

        pieces = []
        for i in range(3, TILES):
            if i + 1 < TILES:
                pieces.append((i + 1, 0))
            pieces.append((i, 1))
        pieces.insert(TURN_STEP, None)
        to_weigh = [(1, 1), (2, 1)] + pieces
        to_quantize = {TURN_STEP + LAG: TILES - 2, TURN_STEP + LAG + 1: TILES - 1}
        steps = 2 * TILES
        for n in range(steps):
            i, b = n // 2, 2 * (n % 2)
            first_bank, second_bank = integrate(i, b), integrate(i, b + 1)
            weighing = to_weigh[n] if n < len(to_weigh) else None
            if weighing:
                weigh(*weighing)
            first = apply_rate(first_bank, b, 0, BANK)
            if weighing:
                quantize_detected(*weighing)
            if n in to_quantize:
                quantize_cells(to_quantize[n])
            cuts = (0, BANK) if n < steps - 1 else (0, BANK // 2, BANK)
            second = [apply_rate(second_bank, b + 1, c0, c1) for c0, c1 in zip(cuts, cuts[1:])]
            if n < TURN_STEP:
                presort(TILES - TURN_STEP + n)
            score(i, *first)
            if n == TURN_STEP:
                turn(TILES - 2, TILES - 1)
            elif n < len(pieces):
                volts_squared(*pieces[n])
            for part in second:
                score(i, *part)
